import numpy as np, ml_dtypes
CORES = [7,391,135,263,15,399,143,271]
N = 8
import mx_ref
NC = 128
BF = ml_dtypes.bfloat16
def setup_inputs(rng):
    def f(*shape):
        return mx_ref.flush((rng.standard_normal(shape, dtype=np.float32) * np.exp2(rng.integers(-2, 3, shape[:-1] + (1,)))).astype(BF))
    return {"x": f(N, 128, 512), "rt": f(N, 128, 512), "w": f(N, 128, 4 * NC)}
def setup_inputs_blocks(rng):
    d = setup_inputs(rng)
    for k in ("x", "rt", "w"): d[k] = mx_ref.spread(d[k], rng, 4)
    return d
def setup_inputs_wide(rng):
    d = setup_inputs(rng)
    for k in ("x", "rt", "w"): d[k] = mx_ref.flush((d[k].astype(np.float32) * np.exp2(rng.integers(-6, 7, (N, 1, 1))).astype(np.float32)).astype(BF))
    return d
def setup_inputs_near(rng):
    d = setup_inputs(rng); v = d["rt"].astype(np.float32).reshape(N, 128, -1, 4)
    d["rt"] = mx_ref.flush((v[:, :, :1] + v / 64).reshape(d["rt"].shape).astype(BF))
    return d
def setup_inputs_twins(rng):
    d = setup_inputs(rng); v = d["rt"].reshape(N, 128, -1, 4).copy()
    v[:, :, 1] = v[:, :, 0]
    d["rt"] = v.reshape(d["rt"].shape)
    return d
def reference(x, rt, w):
    W = [mx_ref.quantize(w[e]) for e in range(N)]
    y = np.zeros((N, 128, NC), np.float32)
    for j in range(N):
        X = mx_ref.quantize(x[j])
        lg = mx_ref.matmul(X, mx_ref.quantize(rt[j]))[:, :N]
        m = lg.max(axis=1, keepdims=True)
        for e in range(N):
            y[j] = y[j] + (lg[:, e:e + 1] == m) * (mx_ref.matmul(X, W[e]) * m)
    return {"y": y}

@@ -1,0 +1,162 @@
+from concourse.bass import DstId, RemoteDMATransfer
+from concourse.mybir import dt, AluOpType, AxisListType, ActivationFunctionType
+
+N = 8
+NC = 128
+BANK = 512
+ROUTE = ("plane", "cross", "mate")
+EARLY = 1
+
+SCRATCH = {
+    "wb": ("sbuf", [128, 4 * NC], "bfloat16"),
+    "xb": ("sbuf", [128, 512], "bfloat16"),
+    "rb": ("sbuf", [128, 512], "bfloat16"),
+    "wq": ("sbuf", [128, N * NC], "float8_e4m3fn_x4"),
+    "ws": ("sbuf", [128, N * NC], "uint8"),
+    "xq": ("sbuf", [128, 128], "float8_e4m3fn_x4"),
+    "xs": ("sbuf", [128, 128], "uint8"),
+    "rq": ("sbuf", [128, 128], "float8_e4m3fn_x4"),
+    "rs": ("sbuf", [128, 128], "uint8"),
+    "ps": ("psum", [128, (5 + EARLY) * BANK], "float32"),
+    "top": ("sbuf", [128, 4], "float32"),
+    "gate": ("sbuf", [128, N], "float32"),
+    "acc": ("sbuf", [128, NC], "float32"),
+    "term": ("sbuf", [128, N * NC], "float32"),
+}
+SEMAPHORES = (["lw", "lx", "lr", "qw", "qx", "qr", "cp", "cc", "sent", "mr", "vt", "vg", "va", "done"]
+              + ["a%d" % e for e in range(N)] + ["b%d" % e for e in range(N)]
+              + ["m%d" % k for k in range(8)] + ["p%d" % e for e in range(N)])
+
+
+def _peers(core, T, topo):
+    others = [c for c in T.cores if c != core]
+    far = [c for c in others if topo.rack(topo.host(c)) != topo.rack(topo.host(core))
+           and topo.chip(c) == topo.chip(core) and topo.may_write(core, c)]
+    mate = [c for c in others if topo.mates(core, c)]
+    plane = [c for c in others if topo.same_plane(core, c)]
+    cross = [c for c in others if topo.mates(c, plane[0])]
+    return {"far": far[0], "mate": mate[0], "plane": plane[0], "cross": cross[0]}
+
+
+def _plan(core, T, topo):
+    p = _peers(core, T, topo)
+    own, far = T.rank_of(core), T.rank_of(p["far"])
+    if abs(own - far) != 1:
+        raise ValueError("far partners must be neighbours in rank order")
+    dests = [p[t] for t in ROUTE]
+    return {"peers": p, "own": own, "far": far, "lo": min(own, far), "dests": dests,
+            "whole": dests[:len(dests) - EARLY], "late": dests[len(dests) - EARLY:]}
+
+
+def _mask(src, dests, topo):
+    m = topo.mask(src, dests[0])
+    for d in dests[1:]:
+        m &= topo.mask(src, d)
+    return m
+
+
+def _count(src, dests, topo):
+    return bin(_mask(src, dests, topo)).count("1") if dests else 0
+
+
+def rank_program(g, core, T, topo):
+    if T.rank_of(core) is None:
+        return
+    S = T.sem
+    me = _plan(core, T, topo)
+    own, far, lo = me["own"], me["far"], me["lo"]
+
+    def codes(a, n):
+        return T.wq[:, a * NC:(a + n) * NC].bitcast(dt.uint8)
+
+    def planes(a, n):
+        return T.ws[:, a * NC:(a + n) * NC]
+
+    g.sync.dma_start(T.wb[:], T.w[:]).then_inc(S.lw, 16)
+    g.sync.dma_start(T.xb[:], T.x[:]).then_inc(S.lx, 16)
+    g.sync.dma_start(T.rb[:], T.rt[:]).then_inc(S.lr, 16)
+
+    v = g.vector
+    v.wait_ge(S.lw, 16)
+    v.quantize_mx(T.wq[:, own * NC:(own + 1) * NC], T.ws[:, own * NC:(own + 1) * NC], T.wb[:]).then_inc(S.qw, 1)
+    v.wait_ge(S.lx, 16)
+    v.quantize_mx(T.xq[:], T.xs[:], T.xb[:]).then_inc(S.qx, 1)
+    v.wait_ge(S.lr, 16)
+    v.quantize_mx(T.rq[:], T.rs[:], T.rb[:]).then_inc(S.qr, 1)
+
+    left = [0]
+
+    def send(view, a, n, dests, sem):
+        if not dests:
+            return
+        mask = _mask(core, dests, topo)
+        ids = [topo.addr(d, core) for d in dests]
+        if len(dests) == 1:
+            g.remote_dma(out_ap=view(a, n), in_ap=view(a, n), remote_sem=sem, local_sem=S.sent,
+                         pid=ids[0][1], routing_id=ids[0][0], dma_engine_mask=mask)
+        else:
+            g.remote_dma_fused([RemoteDMATransfer(dst_ids=[DstId(rid=r, pnc=p) for r, p in ids], dma_engine_mask=mask,
+                                                  remote_sem=sem, srcs=[view(a, n)], dsts=[view(a, n) for _ in dests])],
+                               local_sem=S.sent)
+        left[0] += bin(mask).count("1")
+
+    cable = [me["peers"]["far"]]
+    from_far = _count(me["peers"]["far"], [core], topo)
+    g.wait_ge(S.qw, 1)
+    send(planes, own, 1, cable, S.cp)
+    send(codes, own, 1, cable, S.cc)
+    send(codes, own, 1, me["late"], S["a%d" % lo])
+    g.wait_ge(S.cp, from_far)
+    send(planes, lo, 2, me["dests"], S["a%d" % lo])
+    g.wait_ge(S.cc, from_far)
+    send(codes, lo, 2, me["whole"], S["a%d" % lo])
+    send(codes, far, 1, me["late"], S["b%d" % lo])
+    g.wait_ge(S.sent, left[0])
+
+    jobs = [([(S.qw, 1), (S.cp, from_far), (S.cc, from_far)], lo, 2)]
+    senders = [_plan(me["peers"][t], T, topo) for t in ROUTE]
+    cores = [me["peers"][t] for t in ROUTE]
+    split = len(ROUTE) - EARLY
+    for c, s in list(zip(cores, senders))[split:]:
+        jobs.append(([(S["a%d" % s["lo"]], _count(c, s["dests"], topo) + _count(c, s["late"], topo))], s["own"], 1))
+    for c, s in list(zip(cores, senders))[:split]:
+        jobs.append(([(S["a%d" % s["lo"]], _count(c, s["dests"], topo) + _count(c, s["whole"], topo))], s["lo"], 2))
+    for c, s in list(zip(cores, senders))[split:]:
+        jobs.append(([(S["b%d" % s["lo"]], _count(c, s["late"], topo))], s["far"], 1))
+
+    t = g.tensor
+    t.wait_ge(S.qx, 1)
+    t.wait_ge(S.qr, 1)
+    t.matmul_mx(T.ps[:, 0:128], T.xq[:], T.xs[:], T.rq[:], T.rs[:], True, True).then_inc(S.mr, 1)
+    for k, (waits, e, n) in enumerate(jobs):
+        for sem, val in waits:
+            t.wait_ge(sem, val)
+        b = (k + 1) * BANK
+        t.matmul_mx(T.ps[:, b:b + n * NC], T.xq[:], T.xs[:], T.wq[:, e * NC:(e + n) * NC], T.ws[:, e * NC:(e + n) * NC],
+                    True, True).then_inc(S["m%d" % k], 1)
+
+    v.wait_ge(S.mr, 1)
+    v.tensor_reduce(T.top[:, 0:1], T.ps[:, 0:N], AxisListType.X, AluOpType.max).then_inc(S.vt, 1)
+    v.wait_ge(S.vt, 1)
+    v.tensor_scalar(T.gate[:, 0:N], T.ps[:, 0:N], T.top[:, 0:1], T.top[:, 0:1],
+                    AluOpType.is_equal, AluOpType.mult).then_inc(S.vg, 1)
+
+    order = [(k, i, e + i) for k, (waits, e, n) in enumerate(jobs) for i in range(n)]
+    g.scalar.wait_ge(S.vg, 1)
+    for pos, (k, i, e) in enumerate(order):
+        if i == 0:
+            g.scalar.wait_ge(S["m%d" % k], 1)
+        b = (k + 1) * BANK + i * NC
+        out = T.acc[:] if pos == 0 else T.term[:, e * NC:(e + 1) * NC]
+        g.scalar.activation(out, T.ps[:, b:b + NC], ActivationFunctionType.Identity, bias=0.0,
+                            scale=T.gate[:, e:e + 1]).then_inc(S["p%d" % e], 1)
+    v.wait_ge(S["p%d" % order[0][2]], 1)
+    for pos, (k, i, e) in enumerate(order[1:]):
+        v.wait_ge(S["p%d" % e], 1)
+        if pos:
+            v.wait_ge(S.va, pos)
+        v.tensor_tensor(T.acc[:], T.acc[:], T.term[:, e * NC:(e + 1) * NC], AluOpType.add).then_inc(S.va, 1)
+
+    g.sync.wait_ge(S.va, N - 1)
+    g.sync.dma_start(T.y[:], T.acc[:]).then_inc(S.done, 16)
+    g.sync.wait_ge(S.done, 16)

@@ -5,7 +5,7 @@ N = 8
 NC = 128
 BANK = 512
 ROUTE = ("plane", "cross", "mate")
-EARLY = 1
+EARLY = 3
 
 SCRATCH = {
     "wb": ("sbuf", [128, 4 * NC], "bfloat16"),
@@ -55,6 +55,11 @@ def _mask(src, dests, topo):
     return m
 
 
+def _halves(m):
+    on = [b for b in range(m.bit_length()) if (m >> b) & 1]
+    return sum(1 << b for b in on[:len(on) // 2]), sum(1 << b for b in on[len(on) // 2:])
+
+
 def _count(src, dests, topo):
     return bin(_mask(src, dests, topo)).count("1") if dests else 0
 
@@ -86,10 +91,11 @@ def rank_program(g, core, T, topo):
 
     left = [0]
 
-    def send(view, a, n, dests, sem):
+    def send(view, a, n, dests, sem, mask=None):
         if not dests:
             return
-        mask = _mask(core, dests, topo)
+        if mask is None:
+            mask = _mask(core, dests, topo)
         ids = [topo.addr(d, core) for d in dests]
         if len(dests) == 1:
             g.remote_dma(out_ap=view(a, n), in_ap=view(a, n), remote_sem=sem, local_sem=S.sent,
@@ -101,19 +107,20 @@ def rank_program(g, core, T, topo):
         left[0] += bin(mask).count("1")
 
     cable = [me["peers"]["far"]]
-    from_far = _count(me["peers"]["far"], [core], topo)
+    half_p, half_c = _halves(_mask(core, cable, topo))
+    far_p, far_c = [bin(h).count("1") for h in _halves(_mask(me["peers"]["far"], [core], topo))]
     g.wait_ge(S.qw, 1)
-    send(planes, own, 1, cable, S.cp)
-    send(codes, own, 1, cable, S.cc)
+    send(planes, own, 1, cable, S.cp, half_p)
+    send(codes, own, 1, cable, S.cc, half_c)
     send(codes, own, 1, me["late"], S["a%d" % lo])
-    g.wait_ge(S.cp, from_far)
+    g.wait_ge(S.cp, far_p)
     send(planes, lo, 2, me["dests"], S["a%d" % lo])
-    g.wait_ge(S.cc, from_far)
+    g.wait_ge(S.cc, far_c)
     send(codes, lo, 2, me["whole"], S["a%d" % lo])
     send(codes, far, 1, me["late"], S["b%d" % lo])
     g.wait_ge(S.sent, left[0])
 
-    jobs = [([(S.qw, 1), (S.cp, from_far), (S.cc, from_far)], lo, 2)]
+    jobs = [([(S.qw, 1), (S.cp, far_p), (S.cc, far_c)], lo, 2)]
     senders = [_plan(me["peers"][t], T, topo) for t in ROUTE]
     cores = [me["peers"][t] for t in ROUTE]
     split = len(ROUTE) - EARLY

from concourse.bass import DstId, RemoteDMATransfer
from concourse.mybir import dt, AluOpType, AxisListType, ActivationFunctionType

N = 8
NC = 128
BANK = 512
ROUTE = ("plane", "cross", "mate")
EARLY = 3

SCRATCH = {
    "wb": ("sbuf", [128, 4 * NC], "bfloat16"),
    "xb": ("sbuf", [128, 512], "bfloat16"),
    "rb": ("sbuf", [128, 512], "bfloat16"),
    "wq": ("sbuf", [128, N * NC], "float8_e4m3fn_x4"),
    "ws": ("sbuf", [128, N * NC], "uint8"),
    "xq": ("sbuf", [128, 128], "float8_e4m3fn_x4"),
    "xs": ("sbuf", [128, 128], "uint8"),
    "rq": ("sbuf", [128, 128], "float8_e4m3fn_x4"),
    "rs": ("sbuf", [128, 128], "uint8"),
    "ps": ("psum", [128, (5 + EARLY) * BANK], "float32"),
    "top": ("sbuf", [128, 4], "float32"),
    "gate": ("sbuf", [128, N], "float32"),
    "acc": ("sbuf", [128, NC], "float32"),
    "term": ("sbuf", [128, N * NC], "float32"),
}
SEMAPHORES = (["lw", "lx", "lr", "qw", "qx", "qr", "cp", "cc", "sent", "mr", "vt", "vg", "va", "done"]
              + ["a%d" % e for e in range(N)] + ["b%d" % e for e in range(N)]
              + ["m%d" % k for k in range(8)] + ["p%d" % e for e in range(N)])


def _peers(core, T, topo):
    others = [c for c in T.cores if c != core]
    far = [c for c in others if topo.rack(topo.host(c)) != topo.rack(topo.host(core))
           and topo.chip(c) == topo.chip(core) and topo.may_write(core, c)]
    mate = [c for c in others if topo.mates(core, c)]
    plane = [c for c in others if topo.same_plane(core, c)]
    cross = [c for c in others if topo.mates(c, plane[0])]
    return {"far": far[0], "mate": mate[0], "plane": plane[0], "cross": cross[0]}


def _plan(core, T, topo):
    p = _peers(core, T, topo)
    own, far = T.rank_of(core), T.rank_of(p["far"])
    if abs(own - far) != 1:
        raise ValueError("far partners must be neighbours in rank order")
    dests = [p[t] for t in ROUTE]
    return {"peers": p, "own": own, "far": far, "lo": min(own, far), "dests": dests,
            "whole": dests[:len(dests) - EARLY], "late": dests[len(dests) - EARLY:]}


def _mask(src, dests, topo):
    m = topo.mask(src, dests[0])
    for d in dests[1:]:
        m &= topo.mask(src, d)
    return m


def _halves(m):
    on = [b for b in range(m.bit_length()) if (m >> b) & 1]
    return sum(1 << b for b in on[:len(on) // 2]), sum(1 << b for b in on[len(on) // 2:])


def _count(src, dests, topo):
    return bin(_mask(src, dests, topo)).count("1") if dests else 0


def rank_program(g, core, T, topo):
    if T.rank_of(core) is None:
        return
    S = T.sem
    me = _plan(core, T, topo)
    own, far, lo = me["own"], me["far"], me["lo"]

    def codes(a, n):
        return T.wq[:, a * NC:(a + n) * NC].bitcast(dt.uint8)

    def planes(a, n):
        return T.ws[:, a * NC:(a + n) * NC]

    g.sync.dma_start(T.wb[:], T.w[:]).then_inc(S.lw, 16)
    g.sync.dma_start(T.xb[:], T.x[:]).then_inc(S.lx, 16)
    g.sync.dma_start(T.rb[:], T.rt[:]).then_inc(S.lr, 16)

    v = g.vector
    v.wait_ge(S.lw, 16)
    v.quantize_mx(T.wq[:, own * NC:(own + 1) * NC], T.ws[:, own * NC:(own + 1) * NC], T.wb[:]).then_inc(S.qw, 1)
    v.wait_ge(S.lx, 16)
    v.quantize_mx(T.xq[:], T.xs[:], T.xb[:]).then_inc(S.qx, 1)
    v.wait_ge(S.lr, 16)
    v.quantize_mx(T.rq[:], T.rs[:], T.rb[:]).then_inc(S.qr, 1)

    left = [0]

    def send(view, a, n, dests, sem, mask=None):
        if not dests:
            return
        if mask is None:
            mask = _mask(core, dests, topo)
        ids = [topo.addr(d, core) for d in dests]
        if len(dests) == 1:
            g.remote_dma(out_ap=view(a, n), in_ap=view(a, n), remote_sem=sem, local_sem=S.sent,
                         pid=ids[0][1], routing_id=ids[0][0], dma_engine_mask=mask)
        else:
            g.remote_dma_fused([RemoteDMATransfer(dst_ids=[DstId(rid=r, pnc=p) for r, p in ids], dma_engine_mask=mask,
                                                  remote_sem=sem, srcs=[view(a, n)], dsts=[view(a, n) for _ in dests])],
                               local_sem=S.sent)
        left[0] += bin(mask).count("1")

    cable = [me["peers"]["far"]]
    half_p, half_c = _halves(_mask(core, cable, topo))
    far_p, far_c = [bin(h).count("1") for h in _halves(_mask(me["peers"]["far"], [core], topo))]
    g.wait_ge(S.qw, 1)
    send(planes, own, 1, cable, S.cp, half_p)
    send(codes, own, 1, cable, S.cc, half_c)
    send(codes, own, 1, me["late"], S["a%d" % lo])
    g.wait_ge(S.cp, far_p)
    send(planes, lo, 2, me["dests"], S["a%d" % lo])
    g.wait_ge(S.cc, far_c)
    send(codes, lo, 2, me["whole"], S["a%d" % lo])
    send(codes, far, 1, me["late"], S["b%d" % lo])
    g.wait_ge(S.sent, left[0])

    jobs = [([(S.qw, 1), (S.cp, far_p), (S.cc, far_c)], lo, 2)]
    senders = [_plan(me["peers"][t], T, topo) for t in ROUTE]
    cores = [me["peers"][t] for t in ROUTE]
    split = len(ROUTE) - EARLY
    for c, s in list(zip(cores, senders))[split:]:
        jobs.append(([(S["a%d" % s["lo"]], _count(c, s["dests"], topo) + _count(c, s["late"], topo))], s["own"], 1))
    for c, s in list(zip(cores, senders))[:split]:
        jobs.append(([(S["a%d" % s["lo"]], _count(c, s["dests"], topo) + _count(c, s["whole"], topo))], s["lo"], 2))
    for c, s in list(zip(cores, senders))[split:]:
        jobs.append(([(S["b%d" % s["lo"]], _count(c, s["late"], topo))], s["far"], 1))

    t = g.tensor
    t.wait_ge(S.qx, 1)
    t.wait_ge(S.qr, 1)
    t.matmul_mx(T.ps[:, 0:128], T.xq[:], T.xs[:], T.rq[:], T.rs[:], True, True).then_inc(S.mr, 1)
    for k, (waits, e, n) in enumerate(jobs):
        for sem, val in waits:
            t.wait_ge(sem, val)
        b = (k + 1) * BANK
        t.matmul_mx(T.ps[:, b:b + n * NC], T.xq[:], T.xs[:], T.wq[:, e * NC:(e + n) * NC], T.ws[:, e * NC:(e + n) * NC],
                    True, True).then_inc(S["m%d" % k], 1)

    v.wait_ge(S.mr, 1)
    v.tensor_reduce(T.top[:, 0:1], T.ps[:, 0:N], AxisListType.X, AluOpType.max).then_inc(S.vt, 1)
    v.wait_ge(S.vt, 1)
    v.tensor_scalar(T.gate[:, 0:N], T.ps[:, 0:N], T.top[:, 0:1], T.top[:, 0:1],
                    AluOpType.is_equal, AluOpType.mult).then_inc(S.vg, 1)

    order = [(k, i, e + i) for k, (waits, e, n) in enumerate(jobs) for i in range(n)]
    g.scalar.wait_ge(S.vg, 1)
    for pos, (k, i, e) in enumerate(order):
        if i == 0:
            g.scalar.wait_ge(S["m%d" % k], 1)
        b = (k + 1) * BANK + i * NC
        out = T.acc[:] if pos == 0 else T.term[:, e * NC:(e + 1) * NC]
        g.scalar.activation(out, T.ps[:, b:b + NC], ActivationFunctionType.Identity, bias=0.0,
                            scale=T.gate[:, e:e + 1]).then_inc(S["p%d" % e], 1)
    v.wait_ge(S["p%d" % order[0][2]], 1)
    for pos, (k, i, e) in enumerate(order[1:]):
        v.wait_ge(S["p%d" % e], 1)
        if pos:
            v.wait_ge(S.va, pos)
        v.tensor_tensor(T.acc[:], T.acc[:], T.term[:, e * NC:(e + 1) * NC], AluOpType.add).then_inc(S.va, 1)

    g.sync.wait_ge(S.va, N - 1)
    g.sync.dma_start(T.y[:], T.acc[:]).then_inc(S.done, 16)
    g.sync.wait_ge(S.done, 16)
